import numpy as np
import ml_dtypes


def mxq(x, axis, fmt="e4m3"):
    dtype, down = {"e4m3": (ml_dtypes.float8_e4m3fn, 7), "e5m2": (ml_dtypes.float8_e5m2, 14)}[fmt]
    v = np.moveaxis(np.asarray(x, np.float32).astype(ml_dtypes.bfloat16).astype(np.float64), axis, -1)
    blocks = v.reshape(v.shape[:-1] + (-1, 32))
    amax = np.abs(blocks).max(-1, keepdims=True)
    byte = np.maximum(np.where(amax > 0, np.frexp(amax)[1] - 1 + 127, 0) - down, 1)
    scale = np.exp2(byte - 127.0)
    codes = (blocks / scale).astype(np.float32).astype(dtype).astype(np.float64)
    return np.moveaxis((codes * scale).reshape(v.shape), -1, axis)


WIDE = False


def mx_kscale(k):
    if not WIDE:
        return np.ones(k)
    levels = np.array([10, -10, 5, -5, 0])
    if k % 512:
        return np.exp2(np.random.permutation(np.resize(levels, k // 32))).repeat(32)
    a = np.empty((k // 512, 16))
    for p in range(k // 512):
        a[p, :8] = np.random.permutation(np.resize(levels, 8))
        for g in range(8):
            far = levels[np.abs(levels - a[p, g]) >= 10]
            a[p, g + 8] = far[np.random.randint(len(far))]
    return np.exp2(a.ravel()).repeat(32)


def f64(x):
    return np.asarray(x).astype(np.float64)


def striped(idx):
    return np.tile(idx.reshape(-1, 16).T, (8, 1)).astype(np.uint16)


def unstriped(offs):
    return offs[:16].T.reshape(-1).astype(np.int64)


def striped8(idx):
    return np.concatenate([x.reshape(-1, 16).T for x in idx]).astype(np.uint16)


def runs(offs, k):
    lists = np.stack([offs[16 * r : 16 * r + 16].T.reshape(-1) for r in range(8)]).astype(np.int64)
    return lists[np.arange(k) % 512 // 64]


def pack_weight(w):
    k, n = w.shape
    w = f64(np.asarray(w, np.float32).astype(ml_dtypes.bfloat16)).reshape(k // 32, 32, n)
    amax = np.abs(w).max(1)
    byte = np.clip(np.where(amax > 0, np.frexp(amax)[1] - 1 + 127 - 7, 1), 1, 254)
    scaled = (w * np.exp2(127.0 - byte)[:, None, :]).reshape(k, n).astype(np.float32)
    words = np.ascontiguousarray(scaled.reshape(k // 512, 128, 4, n).transpose(0, 1, 3, 2)).astype(ml_dtypes.float8_e4m3fn).view(np.uint8)
    return words, np.ascontiguousarray(byte.astype(np.uint8).reshape(k // 512, 16, n))


def unpack_weight(words, scales):
    g, p, n, _ = words.shape
    vals = np.ascontiguousarray(words).view(ml_dtypes.float8_e4m3fn).astype(np.float64) * np.repeat(np.exp2(scales.astype(np.float64) - 127.0), 8, axis=1)[..., None]
    return vals.transpose(0, 1, 3, 2).reshape(g * 512, n)

def planes(y):
    n, m = y.shape
    v = y.astype(np.float32).astype(ml_dtypes.bfloat16).astype(np.float64).reshape(n // 32, 32, m)
    top = np.abs(v).max(1)
    byte = np.clip(np.where(top > 0, np.frexp(top)[1] - 1 + 127 - 7, 1), 1, 254)
    codes = (v * np.exp2(127.0 - byte)[:, None, :]).reshape(n, m).astype(np.float32).astype(ml_dtypes.float8_e4m3fn).view(np.uint8)
    words = codes.reshape(n // 512, 128, 4, m).transpose(0, 1, 3, 2)
    return np.ascontiguousarray(words), np.ascontiguousarray(byte.astype(np.uint8).reshape(n // 512, 16, m))


K, T, S, G, H, W, U = 512, 1024, 256, 2048, 512, 128, 512


def setup_inputs():
    n = np.random.standard_normal
    s = mx_kscale(K)[:, None]
    packed_xT = pack_weight(n((K, T)) * s)
    packed_dT = pack_weight(n((K, G)) / s)
    perm = np.random.permutation(S)
    perm2 = np.random.permutation(U)
    return {
        "x_words": packed_xT[0],
        "x_scales": packed_xT[1],
        "d_words": packed_dT[0],
        "d_scales": packed_dT[1],
        "gs": (np.random.uniform(0.5, 1.5, (K, 1)) * s).astype(np.float32),
        "offs": striped(np.random.permutation(T)[:S]),
        "k1": striped8(np.random.randint(0, G, (8, H))),
        "two": striped(np.random.permutation(T)[:S]),
        "k2": striped8(np.random.randint(0, G, (8, H))),
        "hz": striped8(np.random.randint(0, T, (8, S))),
        "k3": striped8(np.random.randint(0, G, (8, H))),
        "n1": striped(perm[:W]),
        "n2": striped(perm[W:]),
        "n3": striped(np.random.permutation(S)),
        "k4": striped8(np.random.randint(0, G, (8, H))),
        "k5": striped8(np.random.randint(0, G, (8, H))),
        "hy": striped8(np.random.randint(0, T, (8, S))),
        "n4": striped(perm2[:S]),
        "n5": striped(perm2[S:]),
        "n6": striped(np.random.permutation(S)),
        "n7": striped(np.random.permutation(S)),
    }


def reference(x_words, x_scales, d_words, d_scales, gs, offs, k1, two, k2, hz, k3, n1, n2, n3, k4, k5, hy, n4, n5, n6, n7):
    d_k4 = unpack_weight(d_words, d_scales)[np.arange(K)[:, None], runs(k4, K)]
    d_k1 = unpack_weight(d_words, d_scales)[np.arange(K)[:, None], runs(k1, K)]
    xq = unpack_weight(x_words, x_scales)[:, unstriped(offs)]
    d_k2 = unpack_weight(d_words, d_scales)[np.arange(K)[:, None], runs(k2, K)]
    x_two = unpack_weight(x_words, x_scales)[:, unstriped(two)]
    d_k3 = unpack_weight(d_words, d_scales)[np.arange(K)[:, None], runs(k3, K)]
    x_hz = unpack_weight(x_words, x_scales)[np.arange(K)[:, None], runs(hz, K)]
    h = 0.0625 * (d_k1.T @ xq + d_k2.T @ x_two + d_k3.T @ x_hz)
    pa = h[:, unstriped(n1)]
    pb = h[:, unstriped(n2)]
    rb = np.minimum(pa, pb)
    ra = np.maximum(pa, pb)
    ua = np.zeros((H, S))
    ua[:, unstriped(n1)] = ra
    ub = ua.copy()
    ub[:, unstriped(n2)] = rb
    z = f64(gs) * (ub - ub[:, unstriped(n3)])
    d_k5 = unpack_weight(d_words, d_scales)[np.arange(K)[:, None], runs(k5, K)]
    x_hy = unpack_weight(x_words, x_scales)[np.arange(K)[:, None], runs(hy, K)]
    h2 = 0.0625 * ((d_k4.T @ mxq(z, 0, "e4m3") + d_k5.T @ x_hy))
    dn = h2 - h2[:, unstriped(n7)]
    up = np.maximum(h2, h2[:, unstriped(n6)])
    ph = np.zeros((H, U))
    ph[:, unstriped(n4)] = up
    out = ph.copy()
    out[:, unstriped(n5)] = dn
    return (out,) + planes(out)

@@ -1,0 +1,286 @@
+from contextlib import ExitStack
+
+import concourse.mybir as mybir
+
+K, T, S, G, H, W, U = 512, 1024, 256, 2048, 512, 128, 512
+FLOPS = 5 * 2 * K * H * S
+
+F32 = mybir.dt.float32
+BF16 = mybir.dt.bfloat16
+I32 = mybir.dt.int32
+U32 = mybir.dt.uint32
+U16 = mybir.dt.uint16
+U8 = mybir.dt.uint8
+FP8X4 = mybir.dt.float8_e4m3fn_x4
+ALU = mybir.AluOpType
+COPY = mybir.ActivationFunctionType.Copy
+
+P = 128
+PACK = 4
+HALF = H // 2
+SPARE = 16
+SIXTEENTH = 0.0625
+
+
+def tile_picked_mtthzmhorddpagdd_none_po_kernel(
+    tc, x_words, x_scales, d_words, d_scales, gs,
+    offs, k1, two, k2, hz, k3, n1, n2, n3, k4, k5, hy, n4, n5, n6, n7,
+    out_0, out_1, out_2,
+):
+    nc = tc.nc
+    with ExitStack() as ctx:
+        keep = ctx.enter_context(tc.tile_pool(name="keep", bufs=1))
+        psum = ctx.enter_context(tc.psum_pool(name="psum", bufs=1))
+
+        def tile(shape, dtype, name, tag=None):
+            return keep.tile(shape, dtype, name=name, tag=tag or name, align_bytes=64)
+
+        def load_list(name, src):
+            lst = tile(list(src.shape), U16, "list_" + name)
+            nc.sync.dma_start(lst[:], src)
+            return lst
+
+        def gather_codes(out, window, offsets):
+            nc.vector.tensor_copy(out=out, in_=window[:].indirect(offsets))
+
+        def fetch(out, window, offsets):
+            nc.scalar.activation(out=out, in_=window[:].indirect(offsets), func=COPY)
+
+        def put(window, offsets, values):
+            nc.scalar.activation(out=window[:].indirect(offsets), in_=values, func=COPY)
+
+        def place_scale_rows(plane, picked, queues):
+            for e in range(4):
+                src = 16 * (e // 2) + e % 2
+                queues[e % len(queues)].dma_start(
+                    plane[e:P:32, :].bitcast(I32), picked[src:P:32, :].bitcast(I32))
+
+        d_bytes = tile([P, G], U8, "d_bytes")
+        x_bytes = tile([P, T], U8, "x_bytes")
+        nc.vector.memset(d_bytes[:].bitcast(I32), 0)
+        nc.vector.memset(x_bytes[:].bitcast(I32), 0)
+        l_k = [load_list("k1", k1), load_list("k2", k2), load_list("k3", k3)]
+        for table, src in ((d_bytes, d_scales), (x_bytes, x_scales)):
+            rows = src[0].rearrange("(r e) c -> e r c", e=2)
+            for e in range(2):
+                nc.scalar.dma_start(table[e:P:16, :].bitcast(I32), rows[e].bitcast(I32))
+        l_x = [load_list("offs", offs), load_list("two", two), load_list("hz", hz)]
+        x_table = tile([P, T], U32, "x_table")
+        nc.sync.dma_start(x_table[:].bitcast(I32), x_words[0].rearrange("p c r -> p (c r)").bitcast(I32))
+        d_table = tile([P, G], U32, "d_table")
+        nc.sync.dma_start(d_table[:].bitcast(I32), d_words[0].rearrange("p c r -> p (c r)").bitcast(I32))
+        l_n1, l_n2 = load_list("n1", n1), load_list("n2", n2)
+
+        plane_a = tile([P, 3 * HALF + 3 * S], U8, "plane_a")
+        plane_b = tile([P, 3 * HALF], U8, "plane_b")
+        plane_c = tile([P, 2 * H + S], U8, "plane_c")
+        for plane in (plane_a, plane_b, plane_c):
+            nc.vector.memset(plane[:].bitcast(I32), 0)
+        ub = [tile([P, S + SPARE], F32, "ub%d" % a) for a in range(4)]
+        h2 = [tile([P, S + SPARE], F32, "h2_%d" % t) for t in range(4)]
+        for window in ub + h2:
+            nc.vector.memset(window[:, S:], 0.0)
+
+        def half_of(lst, half):
+            cols = HALF // 16
+            return lst[:, half * cols:(half + 1) * cols]
+
+        picked_a = tile([P, 3 * HALF + 3 * S], U8, "picked_a")
+        for i in range(3):
+            gather_codes(picked_a[:, i * HALF:(i + 1) * HALF], d_bytes, half_of(l_k[i], 0))
+        for i in range(3):
+            gather_codes(picked_a[:, 3 * HALF + i * S:3 * HALF + (i + 1) * S], x_bytes, l_x[i][:])
+        place_scale_rows(plane_a, picked_a, (nc.sync, nc.scalar))
+        x_codes = [tile([P, S], U32, "x_codes%d" % i) for i in range(3)]
+        for i in range(3):
+            gather_codes(x_codes[i][:], x_table, l_x[i][:])
+
+        l_n3 = load_list("n3", n3)
+        gain = tile([P, 4], F32, "gain")
+        with nc.allow_non_contiguous_dma(reason="one weight a row"):
+            nc.sync.dma_start(gain[:], gs.rearrange("(a p) o -> p (a o)", p=P))
+        l_k4, l_k5, l_hy = load_list("k4", k4), load_list("k5", k5), load_list("hy", hy)
+        l_n6, l_n7 = load_list("n6", n6), load_list("n7", n7)
+        l_n4, l_n5 = load_list("n4", n4), load_list("n5", n5)
+        minus_gain = tile([P, 4], F32, "minus_gain")
+        nc.scalar.activation(out=minus_gain[:], in_=gain[:], func=COPY, scale=-1.0)
+
+        h_bank = [psum.tile([P, S], F32, name="h_bank%d" % a) for a in range(4)]
+        h = [tile([P, S], F32, "h%d" % a) for a in range(4)]
+
+        def first_products(half, plane, tags):
+            for i in range(3):
+                codes = tile([P, HALF], U32, "d_codes%d_%d" % (half, i), tags[i])
+                gather_codes(codes[:], d_table, half_of(l_k[i], half))
+                for u in range(2):
+                    nc.tensor.matmul_mx(
+                        out=h_bank[2 * half + u][:],
+                        lhsT=codes[:, u * P:(u + 1) * P].bitcast(FP8X4),
+                        lhsT_scale=plane[:, i * HALF + u * P:i * HALF + (u + 1) * P],
+                        rhs=x_codes[i][:].bitcast(FP8X4),
+                        rhs_scale=plane_a[:, 3 * HALF + i * S:3 * HALF + (i + 1) * S],
+                        start=(i == 0), stop=(i == 2))
+
+        pa, pb, ra, rb = {}, {}, {}, {}
+
+        def fetch_pairs(a):
+            pa[a] = tile([P, W], F32, "pa%d" % a)
+            pb[a] = tile([P, W], F32, "pb%d" % a)
+            fetch(pa[a][:], h[a], l_n1[:])
+            fetch(pb[a][:], h[a], l_n2[:])
+
+        def sort_pairs(a):
+            ra[a] = tile([P, W], F32, "ra%d" % a)
+            rb[a] = tile([P, W], F32, "rb%d" % a)
+            nc.vector.tensor_tensor(out=ra[a][:], in0=pa[a][:], in1=pb[a][:], op=ALU.max)
+            nc.vector.tensor_tensor(out=rb[a][:], in0=pa[a][:], in1=pb[a][:], op=ALU.min)
+
+        def put_pairs(a0):
+            for a in (a0, a0 + 1):
+                put(ub[a], l_n1[:], ra[a][:])
+            for a in (a0, a0 + 1):
+                put(ub[a], l_n2[:], rb[a][:])
+
+        z_rows = tile([P, PACK, S], BF16, "z_rows")
+        ub_n3 = {}
+
+        def fetch_partner(a):
+            ub_n3[a] = tile([P, S], F32, "ub_n3_%d" % a)
+            fetch(ub_n3[a][:], ub[a], l_n3[:])
+
+        def make_z(a, queues):
+            weighted = tile([P, S], F32, "weighted%d" % a, ("pa2", "pb2", None, None)[a])
+            nc.vector.tensor_scalar_mul(weighted[:], ub[a][:, :S], gain[:, a:a + 1])
+            z = tile([P, S], BF16, "z%d" % a)
+            nc.vector.scalar_tensor_tensor(
+                out=z[:], in0=ub_n3[a][:], scalar=minus_gain[:, a:a + 1], in1=weighted[:],
+                op0=ALU.mult, op1=ALU.add)
+            for t in range(PACK):
+                queues[t % len(queues)].dma_start(z_rows[32 * a:32 * (a + 1), t, :], z[t:P:PACK, :])
+
+        first_products(0, plane_a, ("first_codes", None, None))
+        picked_b = tile([P, 3 * HALF], U8, "picked_b", "first_codes")
+        for i in range(3):
+            gather_codes(picked_b[:, i * HALF:(i + 1) * HALF], d_bytes, half_of(l_k[i], 1))
+        place_scale_rows(plane_b, picked_b, (nc.sync,))
+        for a in (0, 1):
+            nc.scalar.activation(out=h[a][:], in_=h_bank[a][:], func=COPY, scale=SIXTEENTH)
+        for a in (0, 1):
+            fetch_pairs(a)
+            sort_pairs(a)
+        put_pairs(0)
+        first_products(1, plane_b, ("pa0", "pa1", "pb1"))
+        dealt_bytes = tile([P, 2 * H + S], U8, "dealt_bytes")
+        picked_hy = tile([P, S], U8, "picked_hy", "pa0")
+        gather_codes(picked_hy[:], x_bytes, l_hy[:])
+        for a in (2, 3):
+            nc.vector.tensor_scalar_mul(h[a][:], h_bank[a][:], SIXTEENTH)
+        for a in (2, 3):
+            fetch_pairs(a)
+        picked_k4 = tile([P, H], U8, "picked_k4", "pb1")
+        gather_codes(picked_k4[:], d_bytes, l_k4[:])
+        for a in (2, 3):
+            sort_pairs(a)
+        for a in (0, 1):
+            fetch_partner(a)
+        put_pairs(2)
+        picked_k5 = tile([P, H], U8, "picked_k5", "pa3")
+        gather_codes(picked_k5[:], d_bytes, l_k5[:])
+        for a in (0, 1):
+            make_z(a, (nc.sync,))
+
+        def deal(out, src):
+            nc.vector.tensor_copy(out=out.rearrange("p (t m) -> p m t", t=PACK),
+                                  in_=src.rearrange("p (m t) -> p m t", t=PACK))
+
+        deal(dealt_bytes[:, :H], picked_k4[:])
+        deal(dealt_bytes[:, H:2 * H], picked_k5[:])
+        nc.vector.tensor_copy(out=dealt_bytes[:, 2 * H:].bitcast(I32), in_=picked_hy[:].bitcast(I32))
+        place_scale_rows(plane_c, dealt_bytes, (nc.sync,))
+
+        raw_k4 = tile([P, H], U32, "raw_k4", "pa3")
+        gather_codes(raw_k4[:], d_table, l_k4[:])
+        codes_k4 = tile([P, H], U32, "codes_k4")
+        deal(codes_k4[:].bitcast(I32), raw_k4[:].bitcast(I32))
+        fetch_partner(2)
+        make_z(2, (nc.sync,))
+        fetch_partner(3)
+        make_z(3, (nc.sync, nc.scalar))
+        raw_k5 = tile([P, H], U32, "raw_k5", "ub_n3_3")
+        gather_codes(raw_k5[:], d_table, l_k5[:])
+        codes_hy = tile([P, S], U32, "codes_hy", "weighted3")
+        gather_codes(codes_hy[:], x_table, l_hy[:])
+        codes_k5 = tile([P, H], U32, "codes_k5")
+        deal(codes_k5[:].bitcast(I32), raw_k5[:].bitcast(I32))
+
+        z_in = tile([P, S * PACK], BF16, "z_in")
+        z_in_v = z_in[:].rearrange("p (c i t) -> p c t i", i=4, t=PACK)
+        z_rows_v = z_rows[:].rearrange("p t (c i) -> p c t i", i=4)
+        nc.vector.tensor_copy(out=z_in_v[:, :44], in_=z_rows_v[:, :44])
+        nc.scalar.copy(out=z_in_v[:, 44:], in_=z_rows_v[:, 44:])
+        z_codes = tile([P, S], U32, "z_codes")
+        z_scales = tile([P, S], U8, "z_scales")
+        nc.vector.quantize_mx(out=z_codes[:].bitcast(FP8X4), scales=z_scales[:], in_=z_in[:])
+
+        h2_bank = [psum.tile([P, S], F32, name="h2_bank%d" % t) for t in range(4)]
+        for t in range(4):
+            cols = slice(t * P, (t + 1) * P)
+            nc.tensor.matmul_mx(
+                out=h2_bank[t][:], lhsT=codes_k5[:, cols].bitcast(FP8X4),
+                lhsT_scale=plane_c[:, H + t * P:H + (t + 1) * P],
+                rhs=codes_hy[:].bitcast(FP8X4), rhs_scale=plane_c[:, 2 * H:],
+                start=True, stop=False)
+        for t in range(4):
+            cols = slice(t * P, (t + 1) * P)
+            nc.tensor.matmul_mx(
+                out=h2_bank[t][:], lhsT=codes_k4[:, cols].bitcast(FP8X4), lhsT_scale=plane_c[:, cols],
+                rhs=z_codes[:].bitcast(FP8X4), rhs_scale=z_scales[:],
+                start=False, stop=True)
+
+        nc.scalar.activation(out=h2[0][:, :S], in_=h2_bank[0][:], func=COPY, scale=SIXTEENTH)
+        for t in range(1, 4):
+            nc.vector.tensor_scalar_mul(h2[t][:, :S], h2_bank[t][:], SIXTEENTH)
+
+        page = [tile([P, U], F32, "page%d" % t) for t in range(4)]
+        out_in = tile([P, U * PACK], BF16, "out_in")
+        out_rows = out_0.rearrange("(p t) c -> p t c", t=PACK)
+        up, dn = {}, {}
+
+        def fetch_second(t):
+            h2_n6 = tile([P, S], F32, "h2_n6_%d" % t)
+            h2_n7 = tile([P, S], F32, "h2_n7_%d" % t)
+            fetch(h2_n6[:], h2[t], l_n6[:])
+            fetch(h2_n7[:], h2[t], l_n7[:])
+            up[t] = tile([P, S], F32, "up%d" % t)
+            dn[t] = tile([P, S], F32, "dn%d" % t)
+            nc.vector.tensor_tensor(out=up[t][:], in0=h2[t][:, :S], in1=h2_n6[:], op=ALU.max)
+            nc.vector.tensor_tensor(out=dn[t][:], in0=h2[t][:, :S], in1=h2_n7[:], op=ALU.subtract)
+
+        for t0 in (0, 2):
+            for t in (t0, t0 + 1):
+                fetch_second(t)
+            for t in (t0, t0 + 1):
+                put(page[t], l_n4[:], up[t][:])
+            for t in (t0, t0 + 1):
+                put(page[t], l_n5[:], dn[t][:])
+                queue = nc.scalar if t == 3 else nc.sync
+                queue.dma_start(out_rows[:, t, :], page[t][:])
+                if t < 3:
+                    nc.vector.tensor_copy(
+                        out=out_in[:].rearrange("p (c t) -> p c t", t=PACK)[:, :, t], in_=page[t][:])
+
+        out_codes = tile([P, U], U32, "out_codes")
+        out_scales = tile([P, U], U8, "out_scales")
+        words_out = out_1[0].rearrange("p c r -> p (c r)").bitcast(I32)
+        halves = (slice(0, U // 2), slice(U // 2, U))
+        for cols in halves:
+            nc.vector.tensor_copy(
+                out=out_in[:].rearrange("p (c t) -> p c t", t=PACK)[:, cols, 3], in_=page[3][:, cols])
+        for cols in halves:
+            nc.vector.quantize_mx(
+                out=out_codes[:, cols].bitcast(FP8X4), scales=out_scales[:, cols],
+                in_=out_in[:, PACK * cols.start:PACK * cols.stop])
+            nc.sync.dma_start(words_out[:, cols], out_codes[:, cols].bitcast(I32))
+        for q in range(4):
+            queue = nc.sync if q % 2 else nc.scalar
+            queue.dma_start(out_2[0, 4 * q:4 * q + 4, :].bitcast(I32), out_scales[32 * q:32 * q + 4, :].bitcast(I32))

@@ -1,6 +1,7 @@
 from contextlib import ExitStack
 
 import concourse.mybir as mybir
+from concourse.masks import make_identity
 
 K, T, S, G, H, W, U = 512, 1024, 256, 2048, 512, 128, 512
 FLOPS = 5 * 2 * K * H * S
@@ -43,15 +44,15 @@ def tile_picked_mtthzmhorddpagdd_none_po_kernel(
         def gather_codes(out, window, offsets):
             nc.vector.tensor_copy(out=out, in_=window[:].indirect(offsets))
 
-        def fetch(out, window, offsets):
-            nc.scalar.activation(out=out, in_=window[:].indirect(offsets), func=COPY)
+        def fetch(out, window, offsets, scale=1.0):
+            nc.scalar.activation(out=out, in_=window[:].indirect(offsets), func=COPY, scale=scale)
 
         def put(window, offsets, values):
             nc.scalar.activation(out=window[:].indirect(offsets), in_=values, func=COPY)
 
         def place_scale_rows(plane, picked, queues):
             for e in range(4):
-                src = 16 * (e // 2) + e % 2
+                src = 8 * e
                 queues[e % len(queues)].dma_start(
                     plane[e:P:32, :].bitcast(I32), picked[src:P:32, :].bitcast(I32))
 
@@ -61,9 +62,7 @@ def tile_picked_mtthzmhorddpagdd_none_po_kernel(
         nc.vector.memset(x_bytes[:].bitcast(I32), 0)
         l_k = [load_list("k1", k1), load_list("k2", k2), load_list("k3", k3)]
         for table, src in ((d_bytes, d_scales), (x_bytes, x_scales)):
-            rows = src[0].rearrange("(r e) c -> e r c", e=2)
-            for e in range(2):
-                nc.scalar.dma_start(table[e:P:16, :].bitcast(I32), rows[e].bitcast(I32))
+            nc.scalar.dma_start(table[0:P:8, :].bitcast(I32), src[0].bitcast(I32))
         l_x = [load_list("offs", offs), load_list("two", two), load_list("hz", hz)]
         x_table = tile([P, T], U32, "x_table")
         nc.sync.dma_start(x_table[:].bitcast(I32), x_words[0].rearrange("p c r -> p (c r)").bitcast(I32))
@@ -76,9 +75,9 @@ def tile_picked_mtthzmhorddpagdd_none_po_kernel(
         plane_c = tile([P, 2 * H + S], U8, "plane_c")
         for plane in (plane_a, plane_b, plane_c):
             nc.vector.memset(plane[:].bitcast(I32), 0)
-        ub = [tile([P, S + SPARE], F32, "ub%d" % a) for a in range(4)]
+        ub = [tile([P, S], F32, "ub%d" % a) for a in range(4)]
         h2 = [tile([P, S + SPARE], F32, "h2_%d" % t) for t in range(4)]
-        for window in ub + h2:
+        for window in h2:
             nc.vector.memset(window[:, S:], 0.0)
 
         def half_of(lst, half):
@@ -96,26 +95,24 @@ def tile_picked_mtthzmhorddpagdd_none_po_kernel(
             gather_codes(x_codes[i][:], x_table, l_x[i][:])
 
         l_n3 = load_list("n3", n3)
-        gain = tile([P, 4], F32, "gain")
-        with nc.allow_non_contiguous_dma(reason="one weight a row"):
-            nc.sync.dma_start(gain[:], gs.rearrange("(a p) o -> p (a o)", p=P))
+        identity = tile([P, P], F32, "identity")
+        make_identity(nc, identity[:])
         l_k4, l_k5, l_hy = load_list("k4", k4), load_list("k5", k5), load_list("hy", hy)
         l_n6, l_n7 = load_list("n6", n6), load_list("n7", n7)
         l_n4, l_n5 = load_list("n4", n4), load_list("n5", n5)
-        minus_gain = tile([P, 4], F32, "minus_gain")
-        nc.scalar.activation(out=minus_gain[:], in_=gain[:], func=COPY, scale=-1.0)
 
-        h_bank = [psum.tile([P, S], F32, name="h_bank%d" % a) for a in range(4)]
+        h_bank = [psum.tile([P, S], F32, name="h_bank%d" % a, tag="bank%d" % a) for a in range(4)]
         h = [tile([P, S], F32, "h%d" % a) for a in range(4)]
 
         def first_products(half, plane, tags):
+            codes = [tile([P, HALF], U32, "d_codes%d_%d" % (half, i), tags[i]) for i in range(3)]
             for i in range(3):
-                codes = tile([P, HALF], U32, "d_codes%d_%d" % (half, i), tags[i])
-                gather_codes(codes[:], d_table, half_of(l_k[i], half))
-                for u in range(2):
+                gather_codes(codes[i][:], d_table, half_of(l_k[i], half))
+            passes = [(i, u) for i in range(3) for u in range(2)]
+            for i, u in (passes if half == 0 else sorted(passes, key=lambda iu: iu[1])):
                     nc.tensor.matmul_mx(
                         out=h_bank[2 * half + u][:],
-                        lhsT=codes[:, u * P:(u + 1) * P].bitcast(FP8X4),
+                        lhsT=codes[i][:, u * P:(u + 1) * P].bitcast(FP8X4),
                         lhsT_scale=plane[:, i * HALF + u * P:i * HALF + (u + 1) * P],
                         rhs=x_codes[i][:].bitcast(FP8X4),
                         rhs_scale=plane_a[:, 3 * HALF + i * S:3 * HALF + (i + 1) * S],
@@ -141,105 +138,128 @@ def tile_picked_mtthzmhorddpagdd_none_po_kernel(
             for a in (a0, a0 + 1):
                 put(ub[a], l_n2[:], rb[a][:])
 
-        z_rows = tile([P, PACK, S], BF16, "z_rows")
-        ub_n3 = {}
+        minus_ub_n3 = {}
 
-        def fetch_partner(a):
-            ub_n3[a] = tile([P, S], F32, "ub_n3_%d" % a)
-            fetch(ub_n3[a][:], ub[a], l_n3[:])
+        def fetch_partner(a, jh):
+            minus_ub_n3[a, jh] = tile([P, P], F32, "minus_ub_n3_%d_%d" % (a, jh))
+            fetch(minus_ub_n3[a, jh][:], ub[a], l_n3[:, 8 * jh:8 * (jh + 1)], -1.0)
 
-        def make_z(a, queues):
-            weighted = tile([P, S], F32, "weighted%d" % a, ("pa2", "pb2", None, None)[a])
-            nc.vector.tensor_scalar_mul(weighted[:], ub[a][:, :S], gain[:, a:a + 1])
-            z = tile([P, S], BF16, "z%d" % a)
-            nc.vector.scalar_tensor_tensor(
-                out=z[:], in0=ub_n3[a][:], scalar=minus_gain[:, a:a + 1], in1=weighted[:],
-                op0=ALU.mult, op1=ALU.add)
-            for t in range(PACK):
-                queues[t % len(queues)].dma_start(z_rows[32 * a:32 * (a + 1), t, :], z[t:P:PACK, :])
+        def make_z(blocks, tag):
+            bank = psum.tile([P, len(blocks), P], F32, name="diff_" + tag, tag=tag)
+            terms = [(n, ub[a][:, jh * P:(jh + 1) * P]) for n, (a, jh) in enumerate(blocks)]
+            terms += [(n, minus_ub_n3[block][:]) for n, block in enumerate(blocks)]
+            for m, (n, term) in enumerate(terms):
+                nc.tensor.matmul(out=bank[:, n, :], lhsT=term, rhs=identity[:],
+                                 is_transpose=True, start=(m == 0), stop=(m == len(terms) - 1))
+            a, jh = blocks[0]
+            rows = len(blocks) * P
+            nc.vector.tensor_tensor(
+                out=z_turned[jh][:, :, 32 * a:32 * a + rows // PACK, :].rearrange("j u q e -> j q u e"),
+                in0=bank[:].rearrange("j n (q u e) -> j (n q) u e", u=2, e=2),
+                in1=gain_row[:, a * P:a * P + rows].rearrange("j (q u e) -> j q u e", u=2, e=2),
+                op=ALU.mult)
 
         first_products(0, plane_a, ("first_codes", None, None))
         picked_b = tile([P, 3 * HALF], U8, "picked_b", "first_codes")
         for i in range(3):
             gather_codes(picked_b[:, i * HALF:(i + 1) * HALF], d_bytes, half_of(l_k[i], 1))
         place_scale_rows(plane_b, picked_b, (nc.sync,))
+        gain_row = tile([P, K], F32, "gain_row", "first_codes")
+        nc.sync.dma_start(gain_row[:], gs.rearrange("k o -> (o k)").partition_broadcast(P))
         for a in (0, 1):
             nc.scalar.activation(out=h[a][:], in_=h_bank[a][:], func=COPY, scale=SIXTEENTH)
         for a in (0, 1):
             fetch_pairs(a)
             sort_pairs(a)
         put_pairs(0)
-        first_products(1, plane_b, ("pa0", "pa1", "pb1"))
-        dealt_bytes = tile([P, 2 * H + S], U8, "dealt_bytes")
-        picked_hy = tile([P, S], U8, "picked_hy", "pa0")
-        gather_codes(picked_hy[:], x_bytes, l_hy[:])
-        for a in (2, 3):
-            nc.vector.tensor_scalar_mul(h[a][:], h_bank[a][:], SIXTEENTH)
-        for a in (2, 3):
-            fetch_pairs(a)
-        picked_k4 = tile([P, H], U8, "picked_k4", "pb1")
-        gather_codes(picked_k4[:], d_bytes, l_k4[:])
-        for a in (2, 3):
-            sort_pairs(a)
-        for a in (0, 1):
-            fetch_partner(a)
-        put_pairs(2)
-        picked_k5 = tile([P, H], U8, "picked_k5", "pa3")
-        gather_codes(picked_k5[:], d_bytes, l_k5[:])
-        for a in (0, 1):
-            make_z(a, (nc.sync,))
+        first_products(1, plane_b, ("pa1", "pb1", "ra0"))
+        for jh in range(2):
+            for a in (0, 1):
+                fetch_partner(a, jh)
 
         def deal(out, src):
-            nc.vector.tensor_copy(out=out.rearrange("p (t m) -> p m t", t=PACK),
-                                  in_=src.rearrange("p (m t) -> p m t", t=PACK))
+            nc.vector.tensor_copy(out=out.rearrange("p (t m) -> p m t", m=P), in_=src)
 
-        deal(dealt_bytes[:, :H], picked_k4[:])
-        deal(dealt_bytes[:, H:2 * H], picked_k5[:])
-        nc.vector.tensor_copy(out=dealt_bytes[:, 2 * H:].bitcast(I32), in_=picked_hy[:].bitcast(I32))
+        def by_row(raw):
+            return raw.rearrange("p (m t) -> p m t", t=PACK)
+
+        picked_c = tile([P, 2 * H + S], U8, "picked_c", "ra1")
+        gather_codes(picked_c[:, 2 * H:], x_bytes, l_hy[:])
+        gather_codes(picked_c[:, :H], d_bytes, l_k4[:])
+        gather_codes(picked_c[:, H:2 * H], d_bytes, l_k5[:])
+        dealt_bytes = tile([P, 2 * H + S], U8, "dealt_bytes")
+        deal(dealt_bytes[:, :H], by_row(picked_c[:, :H]))
+        deal(dealt_bytes[:, H:2 * H], by_row(picked_c[:, H:2 * H]))
+        nc.vector.tensor_copy(out=dealt_bytes[:, 2 * H:].bitcast(I32), in_=picked_c[:, 2 * H:].bitcast(I32))
         place_scale_rows(plane_c, dealt_bytes, (nc.sync,))
 
-        raw_k4 = tile([P, H], U32, "raw_k4", "pa3")
-        gather_codes(raw_k4[:], d_table, l_k4[:])
-        codes_k4 = tile([P, H], U32, "codes_k4")
-        deal(codes_k4[:].bitcast(I32), raw_k4[:].bitcast(I32))
-        fetch_partner(2)
-        make_z(2, (nc.sync,))
-        fetch_partner(3)
-        make_z(3, (nc.sync, nc.scalar))
-        raw_k5 = tile([P, H], U32, "raw_k5", "ub_n3_3")
-        gather_codes(raw_k5[:], d_table, l_k5[:])
-        codes_hy = tile([P, S], U32, "codes_hy", "weighted3")
-        gather_codes(codes_hy[:], x_table, l_hy[:])
-        codes_k5 = tile([P, H], U32, "codes_k5")
-        deal(codes_k5[:].bitcast(I32), raw_k5[:].bitcast(I32))
-
+        for a in (2, 3):
+            nc.scalar.activation(out=h[a][:], in_=h_bank[a][:], func=COPY, scale=SIXTEENTH)
+        for a in (2, 3):
+            fetch_pairs(a)
+            sort_pairs(a)
+        put_pairs(2)
+        z_turned = [tile([P, 2, P, 2], BF16, "z_turned%d" % jh, ("pb3", "pa3")[jh]) for jh in range(2)]
+        for jh in range(2):
+            make_z([(0, jh), (1, jh)], "bank%d" % (2 + jh))
+        raw = tile([P, 2 * H + S], U32, "raw", "ra2")
+        gather_codes(raw[:, :H], d_table, l_k4[:])
+        gather_codes(raw[:, H:2 * H], d_table, l_k5[:])
+        gather_codes(raw[:, 2 * H:], x_table, l_hy[:])
+        raw_rows = [by_row(raw[:, i * H:(i + 1) * H].bitcast(I32)) for i in range(2)]
+        codes_first = tile([P, 2, P], U32, "codes_first")
+        for i in range(2):
+            nc.vector.tensor_copy(out=codes_first[:, i, :].bitcast(I32), in_=raw_rows[i][:, :, 0])
         z_in = tile([P, S * PACK], BF16, "z_in")
-        z_in_v = z_in[:].rearrange("p (c i t) -> p c t i", i=4, t=PACK)
-        z_rows_v = z_rows[:].rearrange("p t (c i) -> p c t i", i=4)
-        nc.vector.tensor_copy(out=z_in_v[:, :44], in_=z_rows_v[:, :44])
-        nc.scalar.copy(out=z_in_v[:, 44:], in_=z_rows_v[:, 44:])
+        z_in_words = z_in[:].bitcast(F32).rearrange("p (j u) -> p j u", u=2)
         z_codes = tile([P, S], U32, "z_codes")
         z_scales = tile([P, S], U8, "z_scales")
-        nc.vector.quantize_mx(out=z_codes[:].bitcast(FP8X4), scales=z_scales[:], in_=z_in[:])
 
-        h2_bank = [psum.tile([P, S], F32, name="h2_bank%d" % t) for t in range(4)]
-        for t in range(4):
-            cols = slice(t * P, (t + 1) * P)
+        def turn_back(jh, tag):
+            words = z_turned[jh][:].rearrange("j u p e -> j (u p e)").bitcast(F32)
+            bank = psum.tile([P, 2, P], F32, name="back%d" % jh, tag=tag)
+            for u in range(2):
+                nc.tensor.transpose(bank[:, u, :], words[:, u * P:(u + 1) * P], identity[:])
+            nc.scalar.copy(out=z_in_words[:, jh * P:(jh + 1) * P, :], in_=bank[:].rearrange("p u j -> p j u"))
+
+        def quantise_z(jh):
+            cols = slice(jh * P, (jh + 1) * P)
+            nc.vector.quantize_mx(out=z_codes[:, cols].bitcast(FP8X4), scales=z_scales[:, cols],
+                                  in_=z_in[:, PACK * cols.start:PACK * cols.stop])
+
+        for jh in range(2):
+            for a in (2, 3):
+                fetch_partner(a, jh)
+        make_z([(2, 0), (3, 0)], "bank0")
+        make_z([(2, 1)], "bank1")
+        make_z([(3, 1)], "bank2")
+        turn_back(0, "bank3")
+        turn_back(1, "bank1")
+
+        def second_products(bank, t, codes, cols):
+            hy_cols = slice(2 * H + cols.start, 2 * H + cols.stop)
             nc.tensor.matmul_mx(
-                out=h2_bank[t][:], lhsT=codes_k5[:, cols].bitcast(FP8X4),
-                lhsT_scale=plane_c[:, H + t * P:H + (t + 1) * P],
-                rhs=codes_hy[:].bitcast(FP8X4), rhs_scale=plane_c[:, 2 * H:],
+                out=bank[:], lhsT=codes[1].bitcast(FP8X4), lhsT_scale=plane_c[:, H + t * P:H + (t + 1) * P],
+                rhs=raw[:, hy_cols].bitcast(FP8X4), rhs_scale=plane_c[:, hy_cols],
                 start=True, stop=False)
-        for t in range(4):
-            cols = slice(t * P, (t + 1) * P)
             nc.tensor.matmul_mx(
-                out=h2_bank[t][:], lhsT=codes_k4[:, cols].bitcast(FP8X4), lhsT_scale=plane_c[:, cols],
-                rhs=z_codes[:].bitcast(FP8X4), rhs_scale=z_scales[:],
+                out=bank[:], lhsT=codes[0].bitcast(FP8X4), lhsT_scale=plane_c[:, t * P:(t + 1) * P],
+                rhs=z_codes[:, cols].bitcast(FP8X4), rhs_scale=z_scales[:, cols],
                 start=False, stop=True)
 
-        nc.scalar.activation(out=h2[0][:, :S], in_=h2_bank[0][:], func=COPY, scale=SIXTEENTH)
+        for jh in range(2):
+            cols = slice(jh * P, (jh + 1) * P)
+            quantise_z(jh)
+            bank = psum.tile([P, P], F32, name="h2_first%d" % jh, tag="bank%d" % (4 + jh))
+            second_products(bank, 0, [codes_first[:, i, :] for i in range(2)], cols)
+            nc.scalar.activation(out=h2[0][:, cols], in_=bank[:], func=COPY, scale=SIXTEENTH)
+        codes_rest = tile([P, 2, 3 * P], U32, "codes_rest", "pa3")
+        for i in (1, 0):
+            deal(codes_rest[:, i, :].bitcast(I32), raw_rows[i][:, :, 1:])
         for t in range(1, 4):
-            nc.vector.tensor_scalar_mul(h2[t][:, :S], h2_bank[t][:], SIXTEENTH)
+            bank = psum.tile([P, S], F32, name="h2_bank%d" % t, tag="bank%d" % (6, 7, 0)[t - 1])
+            second_products(bank, t, [codes_rest[:, i, (t - 1) * P:t * P] for i in range(2)], slice(0, S))
+            nc.vector.tensor_scalar_mul(h2[t][:, :S], bank[:], SIXTEENTH)
 
         page = [tile([P, U], F32, "page%d" % t) for t in range(4)]
         out_in = tile([P, U * PACK], BF16, "out_in")

@@ -141,22 +141,23 @@ def tile_picked_mtthzmhorddpagdd_none_po_kernel(
         minus_ub_n3 = {}
 
         def fetch_partner(a, jh):
-            minus_ub_n3[a, jh] = tile([P, P], F32, "minus_ub_n3_%d_%d" % (a, jh))
-            fetch(minus_ub_n3[a, jh][:], ub[a], l_n3[:, 8 * jh:8 * (jh + 1)], -1.0)
+            if jh == 0:
+                minus_ub_n3[a] = tile([P, S], F32, "minus_ub_n3_%d" % a, ("h2", "h3", None, None)[a])
+            fetch(minus_ub_n3[a][:, jh * P:(jh + 1) * P], ub[a], l_n3[:, 8 * jh:8 * (jh + 1)], -1.0)
 
         def make_z(blocks, tag):
             bank = psum.tile([P, len(blocks), P], F32, name="diff_" + tag, tag=tag)
             terms = [(n, ub[a][:, jh * P:(jh + 1) * P]) for n, (a, jh) in enumerate(blocks)]
-            terms += [(n, minus_ub_n3[block][:]) for n, block in enumerate(blocks)]
+            terms += [(n, minus_ub_n3[a][:, jh * P:(jh + 1) * P]) for n, (a, jh) in enumerate(blocks)]
             for m, (n, term) in enumerate(terms):
                 nc.tensor.matmul(out=bank[:, n, :], lhsT=term, rhs=identity[:],
                                  is_transpose=True, start=(m == 0), stop=(m == len(terms) - 1))
             a, jh = blocks[0]
             rows = len(blocks) * P
             nc.vector.tensor_tensor(
-                out=z_turned[jh][:, :, 32 * a:32 * a + rows // PACK, :].rearrange("j u q e -> j q u e"),
-                in0=bank[:].rearrange("j n (q u e) -> j (n q) u e", u=2, e=2),
-                in1=gain_row[:, a * P:a * P + rows].rearrange("j (q u e) -> j q u e", u=2, e=2),
+                out=z_turned[jh][:, a * P:a * P + rows],
+                in0=bank[:].rearrange("j n r -> j (n r)"),
+                in1=gain_row[:, a * P:a * P + rows],
                 op=ALU.mult)
 
         first_products(0, plane_a, ("first_codes", None, None))
@@ -172,10 +173,7 @@ def tile_picked_mtthzmhorddpagdd_none_po_kernel(
             fetch_pairs(a)
             sort_pairs(a)
         put_pairs(0)
-        first_products(1, plane_b, ("pa1", "pb1", "ra0"))
-        for jh in range(2):
-            for a in (0, 1):
-                fetch_partner(a, jh)
+        first_products(1, plane_b, ("pa0", "pb0", "ra0"))
 
         def deal(out, src):
             nc.vector.tensor_copy(out=out.rearrange("p (t m) -> p m t", m=P), in_=src)
@@ -183,23 +181,28 @@ def tile_picked_mtthzmhorddpagdd_none_po_kernel(
         def by_row(raw):
             return raw.rearrange("p (m t) -> p m t", t=PACK)
 
-        picked_c = tile([P, 2 * H + S], U8, "picked_c", "ra1")
+        picked_c = tile([P, 2 * H + S], U8, "picked_c", "pb1")
         gather_codes(picked_c[:, 2 * H:], x_bytes, l_hy[:])
         gather_codes(picked_c[:, :H], d_bytes, l_k4[:])
         gather_codes(picked_c[:, H:2 * H], d_bytes, l_k5[:])
-        dealt_bytes = tile([P, 2 * H + S], U8, "dealt_bytes")
-        deal(dealt_bytes[:, :H], by_row(picked_c[:, :H]))
-        deal(dealt_bytes[:, H:2 * H], by_row(picked_c[:, H:2 * H]))
-        nc.vector.tensor_copy(out=dealt_bytes[:, 2 * H:].bitcast(I32), in_=picked_c[:, 2 * H:].bitcast(I32))
-        place_scale_rows(plane_c, dealt_bytes, (nc.sync,))
-
         for a in (2, 3):
             nc.scalar.activation(out=h[a][:], in_=h_bank[a][:], func=COPY, scale=SIXTEENTH)
         for a in (2, 3):
             fetch_pairs(a)
             sort_pairs(a)
+        fetch_partner(0, 0)
+        fetch_partner(1, 0)
+        dealt_bytes = tile([P, 2 * H + S], U8, "dealt_bytes", "pa3")
+        for i in range(2):
+            nc.vector.tensor_copy(
+                out=dealt_bytes[:, i * H:(i + 1) * H].rearrange("p (t m) -> p t m", t=PACK),
+                in_=picked_c[:, i * H:(i + 1) * H].rearrange("p (m t) -> p t m", t=PACK))
+        nc.vector.tensor_copy(out=dealt_bytes[:, 2 * H:].bitcast(I32), in_=picked_c[:, 2 * H:].bitcast(I32))
+        place_scale_rows(plane_c, dealt_bytes, (nc.sync,))
+        fetch_partner(0, 1)
+        fetch_partner(1, 1)
         put_pairs(2)
-        z_turned = [tile([P, 2, P, 2], BF16, "z_turned%d" % jh, ("pb3", "pa3")[jh]) for jh in range(2)]
+        z_turned = [tile([P, K], BF16, "z_turned%d" % jh) for jh in range(2)]
         for jh in range(2):
             make_z([(0, jh), (1, jh)], "bank%d" % (2 + jh))
         raw = tile([P, 2 * H + S], U32, "raw", "ra2")
@@ -216,10 +219,10 @@ def tile_picked_mtthzmhorddpagdd_none_po_kernel(
         z_scales = tile([P, S], U8, "z_scales")
 
         def turn_back(jh, tag):
-            words = z_turned[jh][:].rearrange("j u p e -> j (u p e)").bitcast(F32)
+            words = z_turned[jh][:].bitcast(F32)
             bank = psum.tile([P, 2, P], F32, name="back%d" % jh, tag=tag)
             for u in range(2):
-                nc.tensor.transpose(bank[:, u, :], words[:, u * P:(u + 1) * P], identity[:])
+                nc.tensor.transpose(bank[:, u, :], words[:, u::2], identity[:])
             nc.scalar.copy(out=z_in_words[:, jh * P:(jh + 1) * P, :], in_=bank[:].rearrange("p u j -> p j u"))
 
         def quantise_z(jh):
@@ -253,10 +256,10 @@ def tile_picked_mtthzmhorddpagdd_none_po_kernel(
             bank = psum.tile([P, P], F32, name="h2_first%d" % jh, tag="bank%d" % (4 + jh))
             second_products(bank, 0, [codes_first[:, i, :] for i in range(2)], cols)
             nc.scalar.activation(out=h2[0][:, cols], in_=bank[:], func=COPY, scale=SIXTEENTH)
-        codes_rest = tile([P, 2, 3 * P], U32, "codes_rest", "pa3")
+        codes_rest = tile([P, 2, 3 * P], U32, "codes_rest", "z_turned1")
         for i in (1, 0):
             deal(codes_rest[:, i, :].bitcast(I32), raw_rows[i][:, :, 1:])
-        for t in range(1, 4):
+        for t in (2, 1, 3):
             bank = psum.tile([P, S], F32, name="h2_bank%d" % t, tag="bank%d" % (6, 7, 0)[t - 1])
             second_products(bank, t, [codes_rest[:, i, (t - 1) * P:t * P] for i in range(2)], slice(0, S))
             nc.vector.tensor_scalar_mul(h2[t][:, :S], bank[:], SIXTEENTH)
@@ -276,12 +279,12 @@ def tile_picked_mtthzmhorddpagdd_none_po_kernel(
             nc.vector.tensor_tensor(out=up[t][:], in0=h2[t][:, :S], in1=h2_n6[:], op=ALU.max)
             nc.vector.tensor_tensor(out=dn[t][:], in0=h2[t][:, :S], in1=h2_n7[:], op=ALU.subtract)
 
-        for t0 in (0, 2):
-            for t in (t0, t0 + 1):
+        for pair in ((0, 2), (1, 3)):
+            for t in pair:
                 fetch_second(t)
-            for t in (t0, t0 + 1):
+            for t in pair:
                 put(page[t], l_n4[:], up[t][:])
-            for t in (t0, t0 + 1):
+            for t in pair:
                 put(page[t], l_n5[:], dn[t][:])
                 queue = nc.scalar if t == 3 else nc.sync
                 queue.dma_start(out_rows[:, t, :], page[t][:])
@@ -293,9 +296,10 @@ def tile_picked_mtthzmhorddpagdd_none_po_kernel(
         out_scales = tile([P, U], U8, "out_scales")
         words_out = out_1[0].rearrange("p c r -> p (c r)").bitcast(I32)
         halves = (slice(0, U // 2), slice(U // 2, U))
-        for cols in halves:
-            nc.vector.tensor_copy(
-                out=out_in[:].rearrange("p (c t) -> p c t", t=PACK)[:, cols, 3], in_=page[3][:, cols])
+        last_rows = out_in[:].rearrange("p (c t) -> p c t", t=PACK)[:, :, 3]
+        nc.scalar.copy(out=last_rows[:, 352:], in_=page[3][:, 352:])
+        for cols in (slice(0, 256), slice(256, 352)):
+            nc.vector.tensor_copy(out=last_rows[:, cols], in_=page[3][:, cols])
         for cols in halves:
             nc.vector.quantize_mx(
                 out=out_codes[:, cols].bitcast(FP8X4), scales=out_scales[:, cols],

@@ -175,12 +175,6 @@ def tile_picked_mtthzmhorddpagdd_none_po_kernel(
         put_pairs(0)
         first_products(1, plane_b, ("pa0", "pb0", "ra0"))
 
-        def deal(out, src):
-            nc.vector.tensor_copy(out=out.rearrange("p (t m) -> p m t", m=P), in_=src)
-
-        def by_row(raw):
-            return raw.rearrange("p (m t) -> p m t", t=PACK)
-
         picked_c = tile([P, 2 * H + S], U8, "picked_c", "pb1")
         gather_codes(picked_c[:, 2 * H:], x_bytes, l_hy[:])
         gather_codes(picked_c[:, :H], d_bytes, l_k4[:])
@@ -209,10 +203,11 @@ def tile_picked_mtthzmhorddpagdd_none_po_kernel(
         gather_codes(raw[:, :H], d_table, l_k4[:])
         gather_codes(raw[:, H:2 * H], d_table, l_k5[:])
         gather_codes(raw[:, 2 * H:], x_table, l_hy[:])
-        raw_rows = [by_row(raw[:, i * H:(i + 1) * H].bitcast(I32)) for i in range(2)]
-        codes_first = tile([P, 2, P], U32, "codes_first")
+        codes = tile([P, 2, H], U32, "codes")
         for i in range(2):
-            nc.vector.tensor_copy(out=codes_first[:, i, :].bitcast(I32), in_=raw_rows[i][:, :, 0])
+            nc.vector.tensor_copy(
+                out=codes[:, i, :].bitcast(I32).rearrange("p (t c i) -> p c t i", t=PACK, i=4),
+                in_=raw[:, i * H:(i + 1) * H].bitcast(I32).rearrange("p (c i t) -> p c t i", t=PACK, i=4))
         z_in = tile([P, S * PACK], BF16, "z_in")
         z_in_words = z_in[:].bitcast(F32).rearrange("p (j u) -> p j u", u=2)
         z_codes = tile([P, S], U32, "z_codes")
@@ -239,14 +234,14 @@ def tile_picked_mtthzmhorddpagdd_none_po_kernel(
         turn_back(0, "bank3")
         turn_back(1, "bank1")
 
-        def second_products(bank, t, codes, cols):
+        def second_products(bank, t, cols):
             hy_cols = slice(2 * H + cols.start, 2 * H + cols.stop)
             nc.tensor.matmul_mx(
-                out=bank[:], lhsT=codes[1].bitcast(FP8X4), lhsT_scale=plane_c[:, H + t * P:H + (t + 1) * P],
+                out=bank[:], lhsT=codes[:, 1, t * P:(t + 1) * P].bitcast(FP8X4), lhsT_scale=plane_c[:, H + t * P:H + (t + 1) * P],
                 rhs=raw[:, hy_cols].bitcast(FP8X4), rhs_scale=plane_c[:, hy_cols],
                 start=True, stop=False)
             nc.tensor.matmul_mx(
-                out=bank[:], lhsT=codes[0].bitcast(FP8X4), lhsT_scale=plane_c[:, t * P:(t + 1) * P],
+                out=bank[:], lhsT=codes[:, 0, t * P:(t + 1) * P].bitcast(FP8X4), lhsT_scale=plane_c[:, t * P:(t + 1) * P],
                 rhs=z_codes[:, cols].bitcast(FP8X4), rhs_scale=z_scales[:, cols],
                 start=False, stop=True)
 
@@ -254,14 +249,11 @@ def tile_picked_mtthzmhorddpagdd_none_po_kernel(
             cols = slice(jh * P, (jh + 1) * P)
             quantise_z(jh)
             bank = psum.tile([P, P], F32, name="h2_first%d" % jh, tag="bank%d" % (4 + jh))
-            second_products(bank, 0, [codes_first[:, i, :] for i in range(2)], cols)
+            second_products(bank, 0, cols)
             nc.scalar.activation(out=h2[0][:, cols], in_=bank[:], func=COPY, scale=SIXTEENTH)
-        codes_rest = tile([P, 2, 3 * P], U32, "codes_rest", "z_turned1")
-        for i in (1, 0):
-            deal(codes_rest[:, i, :].bitcast(I32), raw_rows[i][:, :, 1:])
         for t in (2, 1, 3):
             bank = psum.tile([P, S], F32, name="h2_bank%d" % t, tag="bank%d" % (6, 7, 0)[t - 1])
-            second_products(bank, t, [codes_rest[:, i, (t - 1) * P:t * P] for i in range(2)], slice(0, S))
+            second_products(bank, t, slice(0, S))
             nc.vector.tensor_scalar_mul(h2[t][:, :S], bank[:], SIXTEENTH)
 
         page = [tile([P, U], F32, "page%d" % t) for t in range(4)]
@@ -286,8 +278,7 @@ def tile_picked_mtthzmhorddpagdd_none_po_kernel(
                 put(page[t], l_n4[:], up[t][:])
             for t in pair:
                 put(page[t], l_n5[:], dn[t][:])
-                queue = nc.scalar if t == 3 else nc.sync
-                queue.dma_start(out_rows[:, t, :], page[t][:])
+                nc.sync.dma_start(out_rows[:, t, :], page[t][:])
                 if t < 3:
                     nc.vector.tensor_copy(
                         out=out_in[:].rearrange("p (c t) -> p c t", t=PACK)[:, :, t], in_=page[t][:])

from contextlib import ExitStack

import concourse.mybir as mybir
from concourse.masks import make_identity

K, T, S, G, H, W, U = 512, 1024, 256, 2048, 512, 128, 512
FLOPS = 5 * 2 * K * H * S

F32 = mybir.dt.float32
BF16 = mybir.dt.bfloat16
I32 = mybir.dt.int32
U32 = mybir.dt.uint32
U16 = mybir.dt.uint16
U8 = mybir.dt.uint8
FP8X4 = mybir.dt.float8_e4m3fn_x4
ALU = mybir.AluOpType
COPY = mybir.ActivationFunctionType.Copy

P = 128
PACK = 4
HALF = H // 2
SPARE = 16
SIXTEENTH = 0.0625


def tile_picked_mtthzmhorddpagdd_none_po_kernel(
    tc, x_words, x_scales, d_words, d_scales, gs,
    offs, k1, two, k2, hz, k3, n1, n2, n3, k4, k5, hy, n4, n5, n6, n7,
    out_0, out_1, out_2,
):
    nc = tc.nc
    with ExitStack() as ctx:
        keep = ctx.enter_context(tc.tile_pool(name="keep", bufs=1))
        psum = ctx.enter_context(tc.psum_pool(name="psum", bufs=1))

        def tile(shape, dtype, name, tag=None):
            return keep.tile(shape, dtype, name=name, tag=tag or name, align_bytes=64)

        def load_list(name, src):
            lst = tile(list(src.shape), U16, "list_" + name)
            nc.sync.dma_start(lst[:], src)
            return lst

        def gather_codes(out, window, offsets):
            nc.vector.tensor_copy(out=out, in_=window[:].indirect(offsets))

        def fetch(out, window, offsets, scale=1.0):
            nc.scalar.activation(out=out, in_=window[:].indirect(offsets), func=COPY, scale=scale)

        def put(window, offsets, values):
            nc.scalar.activation(out=window[:].indirect(offsets), in_=values, func=COPY)

        def place_scale_rows(plane, picked, queues):
            for e in range(4):
                src = 8 * e
                queues[e % len(queues)].dma_start(
                    plane[e:P:32, :].bitcast(I32), picked[src:P:32, :].bitcast(I32))

        d_bytes = tile([P, G], U8, "d_bytes")
        x_bytes = tile([P, T], U8, "x_bytes")
        nc.vector.memset(d_bytes[:].bitcast(I32), 0)
        nc.vector.memset(x_bytes[:].bitcast(I32), 0)
        l_k = [load_list("k1", k1), load_list("k2", k2), load_list("k3", k3)]
        for table, src in ((d_bytes, d_scales), (x_bytes, x_scales)):
            nc.scalar.dma_start(table[0:P:8, :].bitcast(I32), src[0].bitcast(I32))
        l_x = [load_list("offs", offs), load_list("two", two), load_list("hz", hz)]
        x_table = tile([P, T], U32, "x_table")
        nc.sync.dma_start(x_table[:].bitcast(I32), x_words[0].rearrange("p c r -> p (c r)").bitcast(I32))
        d_table = tile([P, G], U32, "d_table")
        nc.sync.dma_start(d_table[:].bitcast(I32), d_words[0].rearrange("p c r -> p (c r)").bitcast(I32))
        l_n1, l_n2 = load_list("n1", n1), load_list("n2", n2)

        plane_a = tile([P, 3 * HALF + 3 * S], U8, "plane_a")
        plane_b = tile([P, 3 * HALF], U8, "plane_b")
        plane_c = tile([P, 2 * H + S], U8, "plane_c")
        for plane in (plane_a, plane_b, plane_c):
            nc.vector.memset(plane[:].bitcast(I32), 0)
        ub = [tile([P, S], F32, "ub%d" % a) for a in range(4)]
        h2 = [tile([P, S + SPARE], F32, "h2_%d" % t) for t in range(4)]
        for window in h2:
            nc.vector.memset(window[:, S:], 0.0)

        def half_of(lst, half):
            cols = HALF // 16
            return lst[:, half * cols:(half + 1) * cols]

        picked_a = tile([P, 3 * HALF + 3 * S], U8, "picked_a")
        for i in range(3):
            gather_codes(picked_a[:, i * HALF:(i + 1) * HALF], d_bytes, half_of(l_k[i], 0))
        for i in range(3):
            gather_codes(picked_a[:, 3 * HALF + i * S:3 * HALF + (i + 1) * S], x_bytes, l_x[i][:])
        place_scale_rows(plane_a, picked_a, (nc.sync, nc.scalar))
        x_codes = [tile([P, S], U32, "x_codes%d" % i) for i in range(3)]
        for i in range(3):
            gather_codes(x_codes[i][:], x_table, l_x[i][:])

        l_n3 = load_list("n3", n3)
        identity = tile([P, P], F32, "identity")
        make_identity(nc, identity[:])
        l_k4, l_k5, l_hy = load_list("k4", k4), load_list("k5", k5), load_list("hy", hy)
        l_n6, l_n7 = load_list("n6", n6), load_list("n7", n7)
        l_n4, l_n5 = load_list("n4", n4), load_list("n5", n5)

        h_bank = [psum.tile([P, S], F32, name="h_bank%d" % a, tag="bank%d" % a) for a in range(4)]
        h = [tile([P, S], F32, "h%d" % a) for a in range(4)]

        def first_products(half, plane, tags):
            codes = [tile([P, HALF], U32, "d_codes%d_%d" % (half, i), tags[i]) for i in range(3)]
            for i in range(3):
                gather_codes(codes[i][:], d_table, half_of(l_k[i], half))
            passes = [(i, u) for i in range(3) for u in range(2)]
            for i, u in (passes if half == 0 else sorted(passes, key=lambda iu: iu[1])):
                    nc.tensor.matmul_mx(
                        out=h_bank[2 * half + u][:],
                        lhsT=codes[i][:, u * P:(u + 1) * P].bitcast(FP8X4),
                        lhsT_scale=plane[:, i * HALF + u * P:i * HALF + (u + 1) * P],
                        rhs=x_codes[i][:].bitcast(FP8X4),
                        rhs_scale=plane_a[:, 3 * HALF + i * S:3 * HALF + (i + 1) * S],
                        start=(i == 0), stop=(i == 2))

        pa, pb, ra, rb = {}, {}, {}, {}

        def fetch_pairs(a):
            pa[a] = tile([P, W], F32, "pa%d" % a)
            pb[a] = tile([P, W], F32, "pb%d" % a)
            fetch(pa[a][:], h[a], l_n1[:])
            fetch(pb[a][:], h[a], l_n2[:])

        def sort_pairs(a):
            ra[a] = tile([P, W], F32, "ra%d" % a)
            rb[a] = tile([P, W], F32, "rb%d" % a)
            nc.vector.tensor_tensor(out=ra[a][:], in0=pa[a][:], in1=pb[a][:], op=ALU.max)
            nc.vector.tensor_tensor(out=rb[a][:], in0=pa[a][:], in1=pb[a][:], op=ALU.min)

        def put_pairs(a0):
            for a in (a0, a0 + 1):
                put(ub[a], l_n1[:], ra[a][:])
            for a in (a0, a0 + 1):
                put(ub[a], l_n2[:], rb[a][:])

        minus_ub_n3 = {}

        def fetch_partner(a, jh):
            if jh == 0:
                minus_ub_n3[a] = tile([P, S], F32, "minus_ub_n3_%d" % a, ("h2", "h3", None, None)[a])
            fetch(minus_ub_n3[a][:, jh * P:(jh + 1) * P], ub[a], l_n3[:, 8 * jh:8 * (jh + 1)], -1.0)

        def make_z(blocks, tag):
            bank = psum.tile([P, len(blocks), P], F32, name="diff_" + tag, tag=tag)
            terms = [(n, ub[a][:, jh * P:(jh + 1) * P]) for n, (a, jh) in enumerate(blocks)]
            terms += [(n, minus_ub_n3[a][:, jh * P:(jh + 1) * P]) for n, (a, jh) in enumerate(blocks)]
            for m, (n, term) in enumerate(terms):
                nc.tensor.matmul(out=bank[:, n, :], lhsT=term, rhs=identity[:],
                                 is_transpose=True, start=(m == 0), stop=(m == len(terms) - 1))
            a, jh = blocks[0]
            rows = len(blocks) * P
            nc.vector.tensor_tensor(
                out=z_turned[jh][:, a * P:a * P + rows],
                in0=bank[:].rearrange("j n r -> j (n r)"),
                in1=gain_row[:, a * P:a * P + rows],
                op=ALU.mult)

        first_products(0, plane_a, ("first_codes", None, None))
        picked_b = tile([P, 3 * HALF], U8, "picked_b", "first_codes")
        for i in range(3):
            gather_codes(picked_b[:, i * HALF:(i + 1) * HALF], d_bytes, half_of(l_k[i], 1))
        place_scale_rows(plane_b, picked_b, (nc.sync,))
        gain_row = tile([P, K], F32, "gain_row", "first_codes")
        nc.sync.dma_start(gain_row[:], gs.rearrange("k o -> (o k)").partition_broadcast(P))
        for a in (0, 1):
            nc.scalar.activation(out=h[a][:], in_=h_bank[a][:], func=COPY, scale=SIXTEENTH)
        for a in (0, 1):
            fetch_pairs(a)
            sort_pairs(a)
        put_pairs(0)
        first_products(1, plane_b, ("pa0", "pb0", "ra0"))

        picked_c = tile([P, 2 * H + S], U8, "picked_c", "pb1")
        gather_codes(picked_c[:, 2 * H:], x_bytes, l_hy[:])
        gather_codes(picked_c[:, :H], d_bytes, l_k4[:])
        gather_codes(picked_c[:, H:2 * H], d_bytes, l_k5[:])
        for a in (2, 3):
            nc.scalar.activation(out=h[a][:], in_=h_bank[a][:], func=COPY, scale=SIXTEENTH)
        for a in (2, 3):
            fetch_pairs(a)
            sort_pairs(a)
        fetch_partner(0, 0)
        fetch_partner(1, 0)
        dealt_bytes = tile([P, 2 * H + S], U8, "dealt_bytes", "pa3")
        for i in range(2):
            nc.vector.tensor_copy(
                out=dealt_bytes[:, i * H:(i + 1) * H].rearrange("p (t m) -> p t m", t=PACK),
                in_=picked_c[:, i * H:(i + 1) * H].rearrange("p (m t) -> p t m", t=PACK))
        nc.vector.tensor_copy(out=dealt_bytes[:, 2 * H:].bitcast(I32), in_=picked_c[:, 2 * H:].bitcast(I32))
        place_scale_rows(plane_c, dealt_bytes, (nc.sync,))
        fetch_partner(0, 1)
        fetch_partner(1, 1)
        put_pairs(2)
        z_turned = [tile([P, K], BF16, "z_turned%d" % jh) for jh in range(2)]
        for jh in range(2):
            make_z([(0, jh), (1, jh)], "bank%d" % (2 + jh))
        raw = tile([P, 2 * H + S], U32, "raw", "ra2")
        gather_codes(raw[:, :H], d_table, l_k4[:])
        gather_codes(raw[:, H:2 * H], d_table, l_k5[:])
        gather_codes(raw[:, 2 * H:], x_table, l_hy[:])
        codes = tile([P, 2, H], U32, "codes")
        for i in range(2):
            nc.vector.tensor_copy(
                out=codes[:, i, :].bitcast(I32).rearrange("p (t c i) -> p c t i", t=PACK, i=4),
                in_=raw[:, i * H:(i + 1) * H].bitcast(I32).rearrange("p (c i t) -> p c t i", t=PACK, i=4))
        z_in = tile([P, S * PACK], BF16, "z_in")
        z_in_words = z_in[:].bitcast(F32).rearrange("p (j u) -> p j u", u=2)
        z_codes = tile([P, S], U32, "z_codes")
        z_scales = tile([P, S], U8, "z_scales")

        def turn_back(jh, tag):
            words = z_turned[jh][:].bitcast(F32)
            bank = psum.tile([P, 2, P], F32, name="back%d" % jh, tag=tag)
            for u in range(2):
                nc.tensor.transpose(bank[:, u, :], words[:, u::2], identity[:])
            nc.scalar.copy(out=z_in_words[:, jh * P:(jh + 1) * P, :], in_=bank[:].rearrange("p u j -> p j u"))

        def quantise_z(jh):
            cols = slice(jh * P, (jh + 1) * P)
            nc.vector.quantize_mx(out=z_codes[:, cols].bitcast(FP8X4), scales=z_scales[:, cols],
                                  in_=z_in[:, PACK * cols.start:PACK * cols.stop])

        for jh in range(2):
            for a in (2, 3):
                fetch_partner(a, jh)
        make_z([(2, 0), (3, 0)], "bank0")
        make_z([(2, 1)], "bank1")
        make_z([(3, 1)], "bank2")
        turn_back(0, "bank3")
        turn_back(1, "bank1")

        def second_products(bank, t, cols):
            hy_cols = slice(2 * H + cols.start, 2 * H + cols.stop)
            nc.tensor.matmul_mx(
                out=bank[:], lhsT=codes[:, 1, t * P:(t + 1) * P].bitcast(FP8X4), lhsT_scale=plane_c[:, H + t * P:H + (t + 1) * P],
                rhs=raw[:, hy_cols].bitcast(FP8X4), rhs_scale=plane_c[:, hy_cols],
                start=True, stop=False)
            nc.tensor.matmul_mx(
                out=bank[:], lhsT=codes[:, 0, t * P:(t + 1) * P].bitcast(FP8X4), lhsT_scale=plane_c[:, t * P:(t + 1) * P],
                rhs=z_codes[:, cols].bitcast(FP8X4), rhs_scale=z_scales[:, cols],
                start=False, stop=True)

        for jh in range(2):
            cols = slice(jh * P, (jh + 1) * P)
            quantise_z(jh)
            bank = psum.tile([P, P], F32, name="h2_first%d" % jh, tag="bank%d" % (4 + jh))
            second_products(bank, 0, cols)
            nc.scalar.activation(out=h2[0][:, cols], in_=bank[:], func=COPY, scale=SIXTEENTH)
        for t in (2, 1, 3):
            bank = psum.tile([P, S], F32, name="h2_bank%d" % t, tag="bank%d" % (6, 7, 0)[t - 1])
            second_products(bank, t, slice(0, S))
            nc.vector.tensor_scalar_mul(h2[t][:, :S], bank[:], SIXTEENTH)

        page = [tile([P, U], F32, "page%d" % t) for t in range(4)]
        out_in = tile([P, U * PACK], BF16, "out_in")
        out_rows = out_0.rearrange("(p t) c -> p t c", t=PACK)
        up, dn = {}, {}

        def fetch_second(t):
            h2_n6 = tile([P, S], F32, "h2_n6_%d" % t)
            h2_n7 = tile([P, S], F32, "h2_n7_%d" % t)
            fetch(h2_n6[:], h2[t], l_n6[:])
            fetch(h2_n7[:], h2[t], l_n7[:])
            up[t] = tile([P, S], F32, "up%d" % t)
            dn[t] = tile([P, S], F32, "dn%d" % t)
            nc.vector.tensor_tensor(out=up[t][:], in0=h2[t][:, :S], in1=h2_n6[:], op=ALU.max)
            nc.vector.tensor_tensor(out=dn[t][:], in0=h2[t][:, :S], in1=h2_n7[:], op=ALU.subtract)

        for pair in ((0, 2), (1, 3)):
            for t in pair:
                fetch_second(t)
            for t in pair:
                put(page[t], l_n4[:], up[t][:])
            for t in pair:
                put(page[t], l_n5[:], dn[t][:])
                nc.sync.dma_start(out_rows[:, t, :], page[t][:])
                if t < 3:
                    nc.vector.tensor_copy(
                        out=out_in[:].rearrange("p (c t) -> p c t", t=PACK)[:, :, t], in_=page[t][:])

        out_codes = tile([P, U], U32, "out_codes")
        out_scales = tile([P, U], U8, "out_scales")
        words_out = out_1[0].rearrange("p c r -> p (c r)").bitcast(I32)
        halves = (slice(0, U // 2), slice(U // 2, U))
        last_rows = out_in[:].rearrange("p (c t) -> p c t", t=PACK)[:, :, 3]
        nc.scalar.copy(out=last_rows[:, 352:], in_=page[3][:, 352:])
        for cols in (slice(0, 256), slice(256, 352)):
            nc.vector.tensor_copy(out=last_rows[:, cols], in_=page[3][:, cols])
        for cols in halves:
            nc.vector.quantize_mx(
                out=out_codes[:, cols].bitcast(FP8X4), scales=out_scales[:, cols],
                in_=out_in[:, PACK * cols.start:PACK * cols.stop])
            nc.sync.dma_start(words_out[:, cols], out_codes[:, cols].bitcast(I32))
        for q in range(4):
            queue = nc.sync if q % 2 else nc.scalar
            queue.dma_start(out_2[0, 4 * q:4 * q + 4, :].bitcast(I32), out_scales[32 * q:32 * q + 4, :].bitcast(I32))
